import numpy as np
CORES = [5,29,101,125,133,157,229,253]
N = 8
R, T = 8192, 2048
HOST = [c // 128 for c in CORES]
G = [[r for r in range(N) if HOST[r] == h] for h in sorted(set(HOST))]
H = len(G); K = [sorted(set(HOST)).index(h) for h in HOST]
def entries(a): return a.T.reshape(-1)
def pack(v, P): return np.ascontiguousarray(np.asarray(v, np.int32).reshape(-1, P).T)
def among(rng, a): return rng.permutation(np.concatenate([a, rng.choice(a, T - len(a))]))
def lists(rng, how):
    O = np.stack([among(rng, np.arange(N)) for g in G])
    if how == "away": O = np.stack([among(rng, [r for r in range(N) if r not in g]) for g in G])
    if how == "home": O = np.stack([among(rng, g) for g in G])
    J = rng.integers(0, R, (H, T)); J[:, rng.integers(T)] = rng.permutation(R)[:H]
    if how == "distinct": O[:], J = rng.integers(N), rng.permutation(R)[:H * T].reshape(H, T)
    if how == "hotrank":
        s = rng.integers(1, H); O[:] = np.array([rng.choice(G[(k + s) % H]) for k in range(H)])[:, None]; J = np.stack([rng.permutation(R)[:T] for g in G])
    I = R * O + J
    if how == "edge":
        C, Q = rng.integers(0, 2 * N, (H, T)), rng.permutation(T)
        C[:, Q[:2 * N]] = np.stack([rng.permutation(2 * N) for g in G]); C[:, Q[2 * N]] = rng.permutation(2 * N)[:H]
        I = R * (C // 2) + (R - 1) * (C % 2)
    return {"idx": np.stack([pack(I[K[r]], 16) for r in range(N)])}
def setup_inputs(rng):
    return dict({"tab": rng.standard_normal((N, 128, R), dtype=np.float32)}, **lists(rng, "uniform"))
def setup_inputs_away(rng):
    d = setup_inputs(rng); d.update(lists(rng, "away"))
    for k in ("tab",): d[k] = (d[k].astype(np.float32) * 1048576.0).astype(d[k].dtype)
    return d
def setup_inputs_distinct(rng):
    d = setup_inputs(rng); d.update(lists(rng, "distinct"))
    for k in ("tab",): d[k] = (d[k].astype(np.float32) * (1 / 1024.0)).astype(d[k].dtype)
    return d
def setup_inputs_edge(rng):
    d = setup_inputs(rng); d.update(lists(rng, "edge"))
    return d
def setup_inputs_home(rng):
    d = setup_inputs(rng); d.update(lists(rng, "home"))
    return d
def setup_inputs_hotrank(rng):
    d = setup_inputs(rng); d.update(lists(rng, "hotrank"))
    return d
def check_inputs(x):
    bad = []
    if x["idx"].min() < 0 or x["idx"].max() >= N * R: bad.append("idx out of range")
    if any((x["idx"][r] != x["idx"][s]).any() for r in range(N) for s in range(r) if HOST[r] == HOST[s]): bad.append("two ranks of one host hold different lists")
    return bad
def reference(tab, idx):
    A = np.concatenate(list(tab), axis=1)
    return {"y": np.stack([A[:, entries(idx[r])] for r in range(N)])}

@@ -1,0 +1,220 @@
+from concourse.bass import DstId, RemoteDMATransfer
+from concourse.mybir import AluOpType, ActivationFunctionType
+
+SCRATCH = {
+    "win": ("sbuf", [128, 8192], "float32"),
+    "part": ("sbuf", [128, 4096], "float32"),
+    "yb": ("sbuf", [128, 2048], "float32"),
+    "list": ("sbuf", [128, 128], "int32"),
+    "tmp": ("sbuf", [128, 128], "int32"),
+    "offs": ("sbuf", [128, 256], "uint16"),
+}
+STEPS = 5
+LOADS = [2048, 2560, 2560, 1024]
+SEMAPHORES = (["ix", "pre", "oth", "sent", "yd", "lst", "nums", "sof", "ra", "rb", "arr", "pick"]
+              + ["t%d" % k for k in range(len(LOADS))] + ["st%d" % k for k in range(STEPS)] + ["yq%d" % k for k in range(4)])
+
+SLOT, FIRST, SECOND, PICK = 0, 1024, 1536, 1792
+
+
+def split(mask, ways):
+    bits = [1 << b for b in range(32) if mask >> b & 1]
+    n = len(bits) // ways
+    return [sum(bits[n * w:n * w + n]) for w in range(ways)]
+
+
+def layout(core, T, topo):
+    cores = T.cores
+    N = len(cores)
+
+    def chipmates(c):
+        near = range(max(0, c - topo.CORES_PER_CHIP), c + topo.CORES_PER_CHIP + 1)
+        return [d for d in near if (topo.host(d), topo.chip(d)) == (topo.host(c), topo.chip(c))]
+
+    here = [r for r in range(N) if (topo.host(cores[r]), topo.chip(cores[r])) == (topo.host(core), topo.chip(core))]
+    if not here:
+        return None
+    r = here[0]
+    own = [q for q in range(N) if topo.host(cores[q]) == topo.host(cores[r])]
+    oth = [q for q in range(N) if q not in own]
+
+    def workers(q):
+        c = cores[q]
+        w = [d for d in chipmates(c) if d != c and all(topo.may_write(d, e) for e in cores)]
+        return sorted(w, key=lambda d: (topo.die(d) == topo.die(c), d))
+
+    W = [workers(q) for q in range(N)]
+
+    def direct(q, ranks):
+        return [p for p in ranks if p != q and topo.may_write(cores[q], cores[p])]
+
+    def relayed(q, ranks):
+        return [p for p in ranks if not topo.may_write(cores[q], cores[p])]
+
+    def jobs(q):
+        mine, rest = (own, oth) if q in own else (oth, own)
+        o, p, s = relayed(q, mine), relayed(q, rest), direct(q, mine)
+        return [((o[0], [0, 1, 2, 3]), (p[0], [2, 3])),
+                ((o[1], [0, 1, 2, 3]), (p[1], [2, 3])),
+                ((s[0], [0, 1]), (p[0], [0, 1])),
+                ((s[0], [2, 3]), (p[1], [0, 1]))]
+
+    return {"r": r, "own": own, "oth": oth, "W": W, "jobs": jobs, "direct": direct, "relayed": relayed}
+
+
+def rank_program(g, core, T, topo):
+    L = layout(core, T, topo)
+    if L is None:
+        return
+    if core == T.cores[L["r"]]:
+        owner(g, core, T, topo, L)
+    elif core in L["W"][L["r"]]:
+        worker(g, core, T, topo, L)
+
+
+def copy(core, topo, dst, mask, sem, src_ap, dst_ap):
+    rid, pid = topo.addr(dst, core)
+    return RemoteDMATransfer(dst_ids=[DstId(rid=rid, pnc=pid)], dma_engine_mask=mask, remote_sem=sem, src=src_ap, dst=dst_ap)
+
+
+def owner(g, core, T, topo, L):
+    S, cores, r, own, oth, W = T.sem, T.cores, L["r"], L["own"], L["oth"], L["W"]
+    i = own.index(r)
+    mine = W[r]
+    far = L["direct"](r, oth)
+    on_mask = topo.mask(core, mine[0])
+    off_mask = topo.mask(core, cores[far[0]])
+    rest_mask = on_mask & ~off_mask
+    o, p, s = L["relayed"](r, own), L["relayed"](r, oth), L["direct"](r, own)
+
+    def col(d):
+        return 512 * own.index(d) if d in own else 2048 + 512 * oth.index(d)
+
+    for k in range(4):
+        g.sync.dma_start(T.list[16 * k:16 * k + 16, :], T.idx[:]).then_inc(S.ix, 16)
+        g.scalar.dma_start(T.list[16 * k + 64:16 * k + 80, :], T.idx[:]).then_inc(S.ix, 16)
+    a = 0
+    for k, n in enumerate(LOADS):
+        if k >= 2:
+            g.sync.wait_ge(S["t%d" % (k - 2)], 16)
+        g.sync.dma_start(T.win[:, a:a + n], T.tab[:, a:a + n]).then_inc(S["t%d" % k], 16)
+        a += n
+
+    v, sc = g.vector, g.scalar
+    v.wait_ge(S.ix, 128)
+    v.tensor_scalar(out=T.tmp[:], in0=T.list[:], scalar1=8191, scalar2=None, op0=AluOpType.bitwise_and).then_inc(S.pre, 1)
+    v.wait_ge(S.pre, 1)
+    v.tensor_copy(out=T.offs[:, 0:128], in_=T.tmp[:]).then_inc(S.pre, 1)
+
+    def window(a, n):
+        return T.win[:, 0:8192].indirect(T.offs[:, a // 16:(a + n) // 16])
+
+    def by_vector(a, n, sem):
+        v.tensor_copy(out=T.part[:, a:a + n], in_=window(a, n)).then_inc(sem, 1)
+
+    def by_scalar(a, n, sem):
+        sc.activation(out=T.part[:, a:a + n], in_=window(a, n), func=ActivationFunctionType.Copy, bias=-0.0, scale=1.0).then_inc(sem, 1)
+
+    for q in (v, sc):
+        q.wait_ge(S.pre, 2)
+        for k in range(len(LOADS)):
+            q.wait_ge(S["t%d" % k], 16)
+    by_vector(col(o[0]), 512, S.st0)
+    by_scalar(col(o[1]), 512, S.st0)
+    by_vector(col(s[0]), 256, S.st1)
+    by_scalar(col(s[0]) + 256, 256, S.st1)
+    v.wait_ge(S.oth, 32)
+    sc.wait_ge(S.oth, 32)
+    by_vector(col(p[0]), 512, S.st2)
+    by_scalar(col(p[1]), 512, S.st2)
+    by_vector(col(r), 512, S.st3)
+    by_scalar(col(far[0]), 512, S.st3)
+    by_vector(col(far[1]), 256, S.st4)
+    by_scalar(col(far[1]) + 256, 256, S.st4)
+
+    g.wait_ge(S.ix, 128)
+    addrs = [topo.addr(w, core) for w in mine]
+    g.remote_dma_fused([RemoteDMATransfer(
+        dst_ids=[DstId(rid=rid, pnc=pid) for rid, pid in addrs], dma_engine_mask=on_mask, remote_sem=S.lst,
+        srcs=[T.list[:, 32 * i:32 * i + 32]], dsts=[T.list[:, 0:32] for w in mine])], local_sem=S.sent)
+
+    def hand(k, mask, sem, a, n, to):
+        return copy(core, topo, mine[k], mask, sem, T.part[:, a:a + n], T.part[:, to:to + n])
+
+    def deliver(d, masks):
+        return [copy(core, topo, W[d][k], masks[k], S.arr, T.part[:, col(d) + 128 * k:col(d) + 128 * k + 128],
+                     T.part[:, SLOT + 128 * r:SLOT + 128 * r + 128]) for k in range(4)]
+
+    h = split(on_mask, 2)
+    g.wait_ge(S.st0, 2)
+    g.remote_dma_fused([hand(0, h[0], S.ra, col(o[0]), 512, FIRST), hand(1, h[1], S.ra, col(o[1]), 512, FIRST)], local_sem=S.sent)
+    g.wait_ge(S.st1, 2)
+    g.remote_dma_fused([hand(2, h[0], S.ra, col(s[0]), 256, FIRST), hand(3, h[1], S.ra, col(s[0]) + 256, 256, FIRST)], local_sem=S.sent)
+    h = split(on_mask, 4)
+    g.wait_ge(S.st2, 2)
+    g.remote_dma_fused([hand(2, h[0], S.rb, col(p[0]), 256, SECOND), hand(0, h[1], S.rb, col(p[0]) + 256, 256, SECOND),
+                        hand(3, h[2], S.rb, col(p[1]), 256, SECOND), hand(1, h[3], S.rb, col(p[1]) + 256, 256, SECOND)], local_sem=S.sent)
+    g.wait_ge(S.st3, 2)
+    g.remote_dma_fused(deliver(far[0], split(off_mask, 4)) + deliver(r, split(rest_mask, 4)), local_sem=S.sent)
+    g.wait_ge(S.st4, 2)
+    g.remote_dma_fused(deliver(far[1], split(off_mask, 4)), local_sem=S.sent)
+
+    order = [i] + [k for k in range(4) if k != i]
+    for n, k in enumerate(order):
+        q = g.sync if n % 2 == 0 else g.scalar
+        q.wait_ge(S["yq%d" % k], 8)
+        q.dma_start(T.y[:, 512 * k:512 * k + 512], T.yb[:, 512 * k:512 * k + 512]).then_inc(S.yd, 16)
+    g.wait_ge(S.sent, 88)
+    g.wait_ge(S.yd, 64)
+
+
+def worker(g, core, T, topo, L):
+    S, cores, r, own, oth, W = T.sem, T.cores, L["r"], L["own"], L["oth"], L["W"]
+    i, k = own.index(r), W[r].index(core)
+    off_mask = topo.mask(core, cores[oth[0]])
+    v = g.vector
+
+    total = 2 * (1 + len(L["direct"](r, oth)))
+    for q in own + oth:
+        if q != r:
+            for pair in L["jobs"](q):
+                total += sum(8 // len(sl) for d, sl in pair if d == r and k in sl)
+
+    g.iota(T.tmp[:, 32:40], [[0, 8]], 0, 1).then_inc(S.nums, 1)
+    g.iota(T.tmp[:, 40:48], [[16, 8]], 0, 0).then_inc(S.nums, 1)
+    v.wait_ge(S.lst, 16)
+    v.tensor_scalar(out=T.tmp[:, 0:32], in0=T.list[:, 0:32], scalar1=8191, scalar2=None, op0=AluOpType.bitwise_and).then_inc(S.pre, 1)
+    v.wait_ge(S.pre, 1)
+    v.tensor_copy(out=T.offs[:, 0:32], in_=T.tmp[:, 0:32]).then_inc(S.pre, 1)
+    v.wait_ge(S.nums, 2)
+    ops = [
+        lambda: v.tensor_scalar(out=T.tmp[:, 48:56], in0=T.tmp[:, 32:40], scalar1=15, scalar2=None, op0=AluOpType.bitwise_and),
+        lambda: v.tensor_tensor(out=T.tmp[:, 56:64], in0=T.tmp[:, 48:56], in1=T.tmp[:, 40:48], op=AluOpType.add),
+        lambda: v.tensor_scalar(out=T.tmp[:, 64:72], in0=T.list[:, 8 * k:8 * k + 8], scalar1=13, scalar2=None, op0=AluOpType.logical_shift_right),
+        lambda: v.tensor_scalar(out=T.tmp[:, 72:80], in0=T.tmp[:, 64:72], scalar1=128, scalar2=None, op0=AluOpType.mult),
+        lambda: v.tensor_tensor(out=T.tmp[:, 80:88], in0=T.tmp[:, 72:80], in1=T.tmp[:, 56:64], op=AluOpType.add),
+        lambda: v.tensor_copy(out=T.offs[:, 32:40], in_=T.tmp[:, 80:88]),
+    ]
+    for n, op in enumerate(ops):
+        op().then_inc(S.sof, 1)
+        v.wait_ge(S.sof, n + 1)
+    v.wait_ge(S.arr, total)
+    v.tensor_copy(out=T.part[:, PICK:PICK + 128], in_=T.part[:, SLOT:SLOT + 1024].indirect(T.offs[:, 32:40])).then_inc(S.pick, 1)
+
+    g.wait_ge(S.pre, 2)
+    d = cores[oth[k]]
+    rid, pid = topo.addr(d, core)
+    g.remote_dma(out_ap=T.offs[:, 128 + 32 * i:160 + 32 * i], in_ap=T.offs[:, 0:32], remote_sem=S.oth, local_sem=S.sent,
+                 pid=pid, routing_id=rid, dma_engine_mask=topo.mask(core, d))
+    incs = (4 if k >= 2 else 8, 4)
+    for (d, sl), sem, base, n in zip(L["jobs"](r)[k], (S.ra, S.rb), (FIRST, SECOND), (8, 4)):
+        g.wait_ge(sem, n)
+        masks = split(off_mask, len(sl))
+        g.remote_dma_fused([copy(core, topo, W[d][e], masks[x], S.arr, T.part[:, base + 128 * x:base + 128 * x + 128],
+                                 T.part[:, SLOT + 128 * r:SLOT + 128 * r + 128]) for x, e in enumerate(sl)], local_sem=S.sent)
+    g.wait_ge(S.pick, 1)
+    a = 512 * i + 128 * k
+    masks = split(off_mask, 4)
+    g.remote_dma_fused([copy(core, topo, cores[q], masks[x], S["yq%d" % i], T.part[:, PICK:PICK + 128], T.yb[:, a:a + 128])
+                        for x, q in enumerate(own)], local_sem=S.sent)
+    g.wait_ge(S.sent, 32)

@@ -9,12 +9,16 @@ SCRATCH = {
     "tmp": ("sbuf", [128, 128], "int32"),
     "offs": ("sbuf", [128, 256], "uint16"),
 }
-STEPS = 5
+STEPS = 7
 LOADS = [2048, 2560, 2560, 1024]
 SEMAPHORES = (["ix", "pre", "oth", "sent", "yd", "lst", "nums", "sof", "ra", "rb", "arr", "pick"]
               + ["t%d" % k for k in range(len(LOADS))] + ["st%d" % k for k in range(STEPS)] + ["yq%d" % k for k in range(4)])
 
 SLOT, FIRST, SECOND, PICK = 0, 1024, 1536, 1792
+
+
+def count(mask):
+    return bin(mask).count("1")
 
 
 def split(mask, ways):
@@ -27,39 +31,56 @@ def layout(core, T, topo):
     cores = T.cores
     N = len(cores)
 
-    def chipmates(c):
-        near = range(max(0, c - topo.CORES_PER_CHIP), c + topo.CORES_PER_CHIP + 1)
-        return [d for d in near if (topo.host(d), topo.chip(d)) == (topo.host(c), topo.chip(c))]
+    def near(c):
+        return range(max(0, c - 2 * topo.CORES_PER_CHIP), c + 2 * topo.CORES_PER_CHIP + 1)
 
-    here = [r for r in range(N) if (topo.host(cores[r]), topo.chip(cores[r])) == (topo.host(core), topo.chip(core))]
-    if not here:
+    def chip(c):
+        return (topo.host(c), topo.chip(c))
+
+    relays, workers = [], []
+    for c in cores:
+        far = [d for d in near(c) if chip(d) == chip(c) or topo.mates(c, d)]
+        able = [d for d in far if d != c and all(topo.may_write(d, e) for e in cores if e != d)]
+        able.sort(key=lambda d: (chip(d) != chip(c), topo.die(d) == topo.die(c), d))
+        here, mate = [d for d in able if chip(d) == chip(c)], [d for d in able if chip(d) != chip(c)]
+        relays.append(here)
+        workers.append([here[0], here[2], mate[0], mate[2]])
+    mine = [r for r in range(N) if core == cores[r] or core in relays[r] or core in workers[r]]
+    if not mine:
         return None
-    r = here[0]
-    own = [q for q in range(N) if topo.host(cores[q]) == topo.host(cores[r])]
-    oth = [q for q in range(N) if q not in own]
+    r = mine[0]
 
-    def workers(q):
-        c = cores[q]
-        w = [d for d in chipmates(c) if d != c and all(topo.may_write(d, e) for e in cores)]
-        return sorted(w, key=lambda d: (topo.die(d) == topo.die(c), d))
+    def host(q):
+        return [p for p in range(N) if topo.host(cores[p]) == topo.host(cores[q])]
 
-    W = [workers(q) for q in range(N)]
+    def kin(q):
+        own = host(q)
+        oth = [p for p in range(N) if p not in own]
 
-    def direct(q, ranks):
-        return [p for p in ranks if p != q and topo.may_write(cores[q], cores[p])]
+        def same(p):
+            return topo.may_write(cores[q], cores[p])
+        return ([p for p in own if not same(p)], [p for p in own if p != q and same(p)],
+                [p for p in oth if not same(p)], [p for p in oth if same(p)])
 
-    def relayed(q, ranks):
-        return [p for p in ranks if not topo.may_write(cores[q], cores[p])]
+    def relay_jobs(q):
+        o, s, p, f = kin(q)
+        s = s[0]
+        return [[(0, FIRST, [(o[0], 0), (o[0], 1), (o[0], 2), (o[0], 3)]), (1, SECOND, [(s, 0), (s, 1)])],
+                [(0, FIRST, [(o[1], 0), (o[1], 1), (o[1], 2), (o[1], 3)]), (1, SECOND, [(s, 2), (s, 3)])],
+                [(0, FIRST, [(p[0], 0), (p[0], 1), (f[0], 2), (f[0], 3)]), (0, FIRST + 512, [(q, 2)])],
+                [(0, FIRST, [(p[1], 0), (p[1], 1), (f[1], 2), (f[1], 3)]), (0, FIRST + 512, [(q, 3)])]]
 
-    def jobs(q):
-        mine, rest = (own, oth) if q in own else (oth, own)
-        o, p, s = relayed(q, mine), relayed(q, rest), direct(q, mine)
-        return [((o[0], [0, 1, 2, 3]), (p[0], [2, 3])),
-                ((o[1], [0, 1, 2, 3]), (p[1], [2, 3])),
-                ((s[0], [0, 1]), (p[0], [0, 1])),
-                ((s[0], [2, 3]), (p[1], [0, 1]))]
+    def own_jobs(q):
+        o, s, p, f = kin(q)
+        return [[(f[0], 0), (f[0], 1), (p[0], 2), (p[0], 3)], [(f[1], 0), (f[1], 1), (p[1], 2), (p[1], 3)], [(q, 0), (q, 1)]]
 
-    return {"r": r, "own": own, "oth": oth, "W": W, "jobs": jobs, "direct": direct, "relayed": relayed}
+    c = cores[r]
+    on = topo.mask(c, relays[r][0])
+    off = topo.mask(c, cores[kin(r)[3][0]])
+    own = host(r)
+    return {"r": r, "own": own, "oth": [p for p in range(N) if p not in own], "R": relays, "W": workers, "kin": kin,
+            "relay_jobs": relay_jobs, "own_jobs": own_jobs, "on": on, "off": off, "rest": on & ~off,
+            "hand": [[on, on] + split(on, 2), split(on & ~off, 2) + [0, 0]]}
 
 
 def rank_program(g, core, T, topo):
@@ -68,27 +89,21 @@ def rank_program(g, core, T, topo):
         return
     if core == T.cores[L["r"]]:
         owner(g, core, T, topo, L)
-    elif core in L["W"][L["r"]]:
-        worker(g, core, T, topo, L)
+    else:
+        helper(g, core, T, topo, L)
 
 
 def copy(core, topo, dst, mask, sem, src_ap, dst_ap):
     rid, pid = topo.addr(dst, core)
-    return RemoteDMATransfer(dst_ids=[DstId(rid=rid, pnc=pid)], dma_engine_mask=mask, remote_sem=sem, src=src_ap, dst=dst_ap)
+    return count(mask), RemoteDMATransfer(dst_ids=[DstId(rid=rid, pnc=pid)], dma_engine_mask=mask, remote_sem=sem, src=src_ap, dst=dst_ap)
 
 
 def owner(g, core, T, topo, L):
-    S, cores, r, own, oth, W = T.sem, T.cores, L["r"], L["own"], L["oth"], L["W"]
+    S, cores, r, own, oth, R, W = T.sem, T.cores, L["r"], L["own"], L["oth"], L["R"], L["W"]
     i = own.index(r)
-    mine = W[r]
-    far = L["direct"](r, oth)
-    on_mask = topo.mask(core, mine[0])
-    off_mask = topo.mask(core, cores[far[0]])
-    rest_mask = on_mask & ~off_mask
-    o, p, s = L["relayed"](r, own), L["relayed"](r, oth), L["direct"](r, own)
-
-    def col(d):
-        return 512 * own.index(d) if d in own else 2048 + 512 * oth.index(d)
+    o, s, p, f = L["kin"](r)
+    s = s[0]
+    relay_jobs, own_jobs = L["relay_jobs"](r), L["own_jobs"](r)
 
     for k in range(4):
         g.sync.dma_start(T.list[16 * k:16 * k + 16, :], T.idx[:]).then_inc(S.ix, 16)
@@ -100,121 +115,146 @@ def owner(g, core, T, topo, L):
         g.sync.dma_start(T.win[:, a:a + n], T.tab[:, a:a + n]).then_inc(S["t%d" % k], 16)
         a += n
 
+    seq = []
+    for job in relay_jobs[:2]:
+        seq += job[0][2]
+    for job in relay_jobs[2:]:
+        seq += job[0][2] + job[1][2]
+    for job in relay_jobs[:2]:
+        seq += job[1][2]
+    for job in own_jobs:
+        seq += job
+    pos = {sl: 128 * n for n, sl in enumerate(seq)}
+
     v, sc = g.vector, g.scalar
     v.wait_ge(S.ix, 128)
     v.tensor_scalar(out=T.tmp[:], in0=T.list[:], scalar1=8191, scalar2=None, op0=AluOpType.bitwise_and).then_inc(S.pre, 1)
     v.wait_ge(S.pre, 1)
     v.tensor_copy(out=T.offs[:, 0:128], in_=T.tmp[:]).then_inc(S.pre, 1)
-
-    def window(a, n):
-        return T.win[:, 0:8192].indirect(T.offs[:, a // 16:(a + n) // 16])
-
-    def by_vector(a, n, sem):
-        v.tensor_copy(out=T.part[:, a:a + n], in_=window(a, n)).then_inc(sem, 1)
-
-    def by_scalar(a, n, sem):
-        sc.activation(out=T.part[:, a:a + n], in_=window(a, n), func=ActivationFunctionType.Copy, bias=-0.0, scale=1.0).then_inc(sem, 1)
-
     for q in (v, sc):
         q.wait_ge(S.pre, 2)
         for k in range(len(LOADS)):
             q.wait_ge(S["t%d" % k], 16)
-    by_vector(col(o[0]), 512, S.st0)
-    by_scalar(col(o[1]), 512, S.st0)
-    by_vector(col(s[0]), 256, S.st1)
-    by_scalar(col(s[0]) + 256, 256, S.st1)
-    v.wait_ge(S.oth, 32)
-    sc.wait_ge(S.oth, 32)
-    by_vector(col(p[0]), 512, S.st2)
-    by_scalar(col(p[1]), 512, S.st2)
-    by_vector(col(r), 512, S.st3)
-    by_scalar(col(far[0]), 512, S.st3)
-    by_vector(col(far[1]), 256, S.st4)
-    by_scalar(col(far[1]) + 256, 256, S.st4)
+    steps = [([(o[0], 0, 2)], [(o[0], 2, 2)]),
+             ([(o[1], 0, 2)], [(o[1], 2, 2)]),
+             ([(r, 2, 1), (p[0], 0, 2), (f[0], 2, 2)], [(r, 3, 1), (p[1], 0, 2), (f[1], 2, 2)]),
+             ([(s, 0, 2)], [(s, 2, 2)]),
+             ([(f[0], 0, 2)], [(p[0], 2, 2)]),
+             ([(f[1], 0, 2)], [(p[1], 2, 2)]),
+             ([(r, 0, 1)], [(r, 1, 1)])]
+    for q, side in ((v, 0), (sc, 1)):
+        waited = False
+        for n, step in enumerate(steps):
+            for d, k, many in step[side]:
+                if d in oth and not waited:
+                    q.wait_ge(S.oth, 32 if i < 2 else 64)
+                    waited = True
+                b = (32 * own.index(d) if d in own else 128 + 32 * oth.index(d)) + 8 * k
+                a = pos[(d, k)]
+                out, src = T.part[:, a:a + 128 * many], T.win[:, 0:8192].indirect(T.offs[:, b:b + 8 * many])
+                if side == 0:
+                    v.tensor_copy(out=out, in_=src).then_inc(S["st%d" % n], 1)
+                else:
+                    sc.activation(out=out, in_=src, func=ActivationFunctionType.Copy, bias=-0.0, scale=1.0).then_inc(S["st%d" % n], 1)
 
+    sent = [0]
+
+    def call(pairs):
+        g.remote_dma_fused([t for n, t in pairs], local_sem=S.sent)
+        sent[0] += sum(n for n, t in pairs)
+
+    def quarter(q, to, mask):
+        b = 32 * own.index(q)
+        ids = [topo.addr(w, core) for w in to]
+        call([(count(mask), RemoteDMATransfer(
+            dst_ids=[DstId(rid=rid, pnc=pid) for rid, pid in ids], dma_engine_mask=mask, remote_sem=S.lst,
+            srcs=[T.list[:, b:b + 32]], dsts=[T.list[:, 0:32] for w in to]))])
+
+    partner = o[sorted([r, s]).index(r)]
     g.wait_ge(S.ix, 128)
-    addrs = [topo.addr(w, core) for w in mine]
-    g.remote_dma_fused([RemoteDMATransfer(
-        dst_ids=[DstId(rid=rid, pnc=pid) for rid, pid in addrs], dma_engine_mask=on_mask, remote_sem=S.lst,
-        srcs=[T.list[:, 32 * i:32 * i + 32]], dsts=[T.list[:, 0:32] for w in mine])], local_sem=S.sent)
+    quarter(r, R[r], L["on"])
+    quarter(partner, W[partner][2:], L["off"])
 
-    def hand(k, mask, sem, a, n, to):
-        return copy(core, topo, mine[k], mask, sem, T.part[:, a:a + n], T.part[:, to:to + n])
+    def hand(k, n):
+        sls = [sl for which, base, job in relay_jobs[k] if which == n for sl in job]
+        a, to, cols = pos[sls[0]], (FIRST, SECOND)[n], 128 * len(sls)
+        return copy(core, topo, R[r][k], L["hand"][n][k], (S.ra, S.rb)[n], T.part[:, a:a + cols], T.part[:, to:to + cols])
 
-    def deliver(d, masks):
-        return [copy(core, topo, W[d][k], masks[k], S.arr, T.part[:, col(d) + 128 * k:col(d) + 128 * k + 128],
-                     T.part[:, SLOT + 128 * r:SLOT + 128 * r + 128]) for k in range(4)]
+    def deliver(job, mask):
+        return [copy(core, topo, W[d][k], m, S.arr, T.part[:, pos[(d, k)]:pos[(d, k)] + 128], T.part[:, SLOT + 128 * r:SLOT + 128 * r + 128])
+                for (d, k), m in zip(job, split(mask, len(job)))]
 
-    h = split(on_mask, 2)
-    g.wait_ge(S.st0, 2)
-    g.remote_dma_fused([hand(0, h[0], S.ra, col(o[0]), 512, FIRST), hand(1, h[1], S.ra, col(o[1]), 512, FIRST)], local_sem=S.sent)
-    g.wait_ge(S.st1, 2)
-    g.remote_dma_fused([hand(2, h[0], S.ra, col(s[0]), 256, FIRST), hand(3, h[1], S.ra, col(s[0]) + 256, 256, FIRST)], local_sem=S.sent)
-    h = split(on_mask, 4)
-    g.wait_ge(S.st2, 2)
-    g.remote_dma_fused([hand(2, h[0], S.rb, col(p[0]), 256, SECOND), hand(0, h[1], S.rb, col(p[0]) + 256, 256, SECOND),
-                        hand(3, h[2], S.rb, col(p[1]), 256, SECOND), hand(1, h[3], S.rb, col(p[1]) + 256, 256, SECOND)], local_sem=S.sent)
-    g.wait_ge(S.st3, 2)
-    g.remote_dma_fused(deliver(far[0], split(off_mask, 4)) + deliver(r, split(rest_mask, 4)), local_sem=S.sent)
-    g.wait_ge(S.st4, 2)
-    g.remote_dma_fused(deliver(far[1], split(off_mask, 4)), local_sem=S.sent)
+    calls = [[hand(0, 0)], [hand(1, 0)], [hand(2, 0), hand(3, 0)], [hand(0, 1), hand(1, 1)],
+             deliver(own_jobs[0], L["off"]), deliver(own_jobs[1], L["off"]), deliver(own_jobs[2], L["rest"])]
+    for n, pairs in enumerate(calls):
+        g.wait_ge(S["st%d" % n], sum(len(x) for x in steps[n]))
+        call(pairs)
 
-    order = [i] + [k for k in range(4) if k != i]
-    for n, k in enumerate(order):
-        q = g.sync if n % 2 == 0 else g.scalar
-        q.wait_ge(S["yq%d" % k], 8)
-        q.dma_start(T.y[:, 512 * k:512 * k + 512], T.yb[:, 512 * k:512 * k + 512]).then_inc(S.yd, 16)
-    g.wait_ge(S.sent, 88)
+    for q, ks in ((g.sync, [i, i ^ 2]), (g.scalar, [i ^ 1, i ^ 3])):
+        for k in ks:
+            q.wait_ge(S["yq%d" % k], 16)
+            q.dma_start(T.y[:, 512 * k:512 * k + 512], T.yb[:, 512 * k:512 * k + 512]).then_inc(S.yd, 16)
+    g.wait_ge(S.sent, sent[0])
     g.wait_ge(S.yd, 64)
 
 
-def worker(g, core, T, topo, L):
-    S, cores, r, own, oth, W = T.sem, T.cores, L["r"], L["own"], L["oth"], L["W"]
-    i, k = own.index(r), W[r].index(core)
-    off_mask = topo.mask(core, cores[oth[0]])
+def helper(g, core, T, topo, L):
+    S, cores, r, own, oth, R, W = T.sem, T.cores, L["r"], L["own"], L["oth"], L["R"], L["W"]
+    i = own.index(r)
+    k = W[r].index(core) if core in W[r] else None
+    j = R[r].index(core) if core in R[r] else None
     v = g.vector
+    sent = [0]
 
-    total = 2 * (1 + len(L["direct"](r, oth)))
-    for q in own + oth:
-        if q != r:
-            for pair in L["jobs"](q):
-                total += sum(8 // len(sl) for d, sl in pair if d == r and k in sl)
+    def call(pairs):
+        g.remote_dma_fused([t for n, t in pairs], local_sem=S.sent)
+        sent[0] += sum(n for n, t in pairs)
 
-    g.iota(T.tmp[:, 32:40], [[0, 8]], 0, 1).then_inc(S.nums, 1)
-    g.iota(T.tmp[:, 40:48], [[16, 8]], 0, 0).then_inc(S.nums, 1)
-    v.wait_ge(S.lst, 16)
+    if k is not None:
+        g.iota(T.tmp[:, 32:40], [[0, 8]], 0, 1).then_inc(S.nums, 1)
+        g.iota(T.tmp[:, 40:48], [[16, 8]], 0, 0).then_inc(S.nums, 1)
+    v.wait_ge(S.lst, count(L["on"]) if j is not None else count(L["off"]))
     v.tensor_scalar(out=T.tmp[:, 0:32], in0=T.list[:, 0:32], scalar1=8191, scalar2=None, op0=AluOpType.bitwise_and).then_inc(S.pre, 1)
     v.wait_ge(S.pre, 1)
     v.tensor_copy(out=T.offs[:, 0:32], in_=T.tmp[:, 0:32]).then_inc(S.pre, 1)
-    v.wait_ge(S.nums, 2)
-    ops = [
-        lambda: v.tensor_scalar(out=T.tmp[:, 48:56], in0=T.tmp[:, 32:40], scalar1=15, scalar2=None, op0=AluOpType.bitwise_and),
-        lambda: v.tensor_tensor(out=T.tmp[:, 56:64], in0=T.tmp[:, 48:56], in1=T.tmp[:, 40:48], op=AluOpType.add),
-        lambda: v.tensor_scalar(out=T.tmp[:, 64:72], in0=T.list[:, 8 * k:8 * k + 8], scalar1=13, scalar2=None, op0=AluOpType.logical_shift_right),
-        lambda: v.tensor_scalar(out=T.tmp[:, 72:80], in0=T.tmp[:, 64:72], scalar1=128, scalar2=None, op0=AluOpType.mult),
-        lambda: v.tensor_tensor(out=T.tmp[:, 80:88], in0=T.tmp[:, 72:80], in1=T.tmp[:, 56:64], op=AluOpType.add),
-        lambda: v.tensor_copy(out=T.offs[:, 32:40], in_=T.tmp[:, 80:88]),
-    ]
-    for n, op in enumerate(ops):
-        op().then_inc(S.sof, 1)
-        v.wait_ge(S.sof, n + 1)
-    v.wait_ge(S.arr, total)
-    v.tensor_copy(out=T.part[:, PICK:PICK + 128], in_=T.part[:, SLOT:SLOT + 1024].indirect(T.offs[:, 32:40])).then_inc(S.pick, 1)
-
+    d, a, n = {(0, 0): (0, 0, 32), (2, 1): (1, 0, 32), (1, None): (2, 0, 16), (3, None): (2, 16, 16),
+               (None, 2): (3, 0, 16), (None, 3): (3, 16, 16)}[(j, k)]
     g.wait_ge(S.pre, 2)
-    d = cores[oth[k]]
-    rid, pid = topo.addr(d, core)
-    g.remote_dma(out_ap=T.offs[:, 128 + 32 * i:160 + 32 * i], in_ap=T.offs[:, 0:32], remote_sem=S.oth, local_sem=S.sent,
-                 pid=pid, routing_id=rid, dma_engine_mask=topo.mask(core, d))
-    incs = (4 if k >= 2 else 8, 4)
-    for (d, sl), sem, base, n in zip(L["jobs"](r)[k], (S.ra, S.rb), (FIRST, SECOND), (8, 4)):
-        g.wait_ge(sem, n)
-        masks = split(off_mask, len(sl))
-        g.remote_dma_fused([copy(core, topo, W[d][e], masks[x], S.arr, T.part[:, base + 128 * x:base + 128 * x + 128],
-                                 T.part[:, SLOT + 128 * r:SLOT + 128 * r + 128]) for x, e in enumerate(sl)], local_sem=S.sent)
-    g.wait_ge(S.pick, 1)
-    a = 512 * i + 128 * k
-    masks = split(off_mask, 4)
-    g.remote_dma_fused([copy(core, topo, cores[q], masks[x], S["yq%d" % i], T.part[:, PICK:PICK + 128], T.yb[:, a:a + 128])
-                        for x, q in enumerate(own)], local_sem=S.sent)
-    g.wait_ge(S.sent, 32)
+    to = 128 + 32 * i + a
+    call([copy(core, topo, cores[oth[d]], L["off"], S.oth, T.offs[:, a:a + n], T.offs[:, to:to + n])])
+
+    if k is not None:
+        v.wait_ge(S.nums, 2)
+        ops = [
+            lambda: v.tensor_scalar(out=T.tmp[:, 48:56], in0=T.tmp[:, 32:40], scalar1=15, scalar2=None, op0=AluOpType.bitwise_and),
+            lambda: v.tensor_tensor(out=T.tmp[:, 56:64], in0=T.tmp[:, 48:56], in1=T.tmp[:, 40:48], op=AluOpType.add),
+            lambda: v.tensor_scalar(out=T.tmp[:, 64:72], in0=T.list[:, 8 * k:8 * k + 8], scalar1=13, scalar2=None, op0=AluOpType.logical_shift_right),
+            lambda: v.tensor_scalar(out=T.tmp[:, 72:80], in0=T.tmp[:, 64:72], scalar1=128, scalar2=None, op0=AluOpType.mult),
+            lambda: v.tensor_tensor(out=T.tmp[:, 80:88], in0=T.tmp[:, 72:80], in1=T.tmp[:, 56:64], op=AluOpType.add),
+            lambda: v.tensor_copy(out=T.offs[:, 32:40], in_=T.tmp[:, 80:88]),
+        ]
+        for n, op in enumerate(ops):
+            op().then_inc(S.sof, 1)
+            v.wait_ge(S.sof, n + 1)
+        total = 0
+        for q in own + oth:
+            for job in L["relay_jobs"](q):
+                total += sum(count(L["off"]) // len(sls) for which, base, sls in job if (r, k) in sls)
+            total += sum(count(L["off"]) // len(sls) for sls in L["own_jobs"](q)[:2] if (r, k) in sls)
+            total += sum(count(L["rest"]) // len(sls) for sls in L["own_jobs"](q)[2:] if (r, k) in sls)
+        v.wait_ge(S.arr, total)
+        v.tensor_copy(out=T.part[:, PICK:PICK + 128], in_=T.part[:, SLOT:SLOT + 1024].indirect(T.offs[:, 32:40])).then_inc(S.pick, 1)
+
+    if j is not None:
+        for which, base, sls in L["relay_jobs"](r)[j]:
+            g.wait_ge((S.ra, S.rb)[which], count(L["hand"][which][j]))
+            call([copy(core, topo, W[d][e], m, S.arr, T.part[:, base + 128 * x:base + 128 * x + 128], T.part[:, SLOT + 128 * r:SLOT + 128 * r + 128])
+                  for x, ((d, e), m) in enumerate(zip(sls, split(L["off"], len(sls))))])
+
+    if k is not None:
+        a = 512 * i + 128 * k
+        g.wait_ge(S.pick, 1)
+        for pair in ((i, i ^ 1), (i ^ 2, i ^ 3)):
+            call([copy(core, topo, cores[own[q]], m, S["yq%d" % i], T.part[:, PICK:PICK + 128], T.yb[:, a:a + 128])
+                  for q, m in zip(pair, split(L["off"], 2))])
+    g.wait_ge(S.sent, sent[0])

@@ -1,6 +1,9 @@
 from concourse.bass import DstId, RemoteDMATransfer
 from concourse.mybir import AluOpType, ActivationFunctionType
 
+WIDTH = [160, 160, 96, 96]
+LOADS = [3840, 4352]
+SLOT, PASS, PICK = 0, 1280, 2560
 SCRATCH = {
     "win": ("sbuf", [128, 8192], "float32"),
     "part": ("sbuf", [128, 4096], "float32"),
@@ -9,78 +12,113 @@ SCRATCH = {
     "tmp": ("sbuf", [128, 128], "int32"),
     "offs": ("sbuf", [128, 256], "uint16"),
 }
-STEPS = 7
-LOADS = [2048, 2560, 2560, 1024]
-SEMAPHORES = (["ix", "pre", "oth", "sent", "yd", "lst", "nums", "sof", "ra", "rb", "arr", "pick"]
-              + ["t%d" % k for k in range(len(LOADS))] + ["st%d" % k for k in range(STEPS)] + ["yq%d" % k for k in range(4)])
-
-SLOT, FIRST, SECOND, PICK = 0, 1024, 1536, 1792
+SEMAPHORES = (["ix", "go", "pre", "oe", "ol", "sent", "yd", "lst", "nums", "sof", "arr", "pick", "h0", "h1", "vs", "ss"]
+              + ["t%d" % k for k in range(len(LOADS))] + ["y%d" % k for k in range(8)])
 
 
 def count(mask):
     return bin(mask).count("1")
 
 
+def bits(mask):
+    return [1 << b for b in range(32) if mask >> b & 1]
+
+
 def split(mask, ways):
-    bits = [1 << b for b in range(32) if mask >> b & 1]
-    n = len(bits) // ways
-    return [sum(bits[n * w:n * w + n]) for w in range(ways)]
+    n = count(mask) // ways
+    return [sum(bits(mask)[n * w:n * w + n]) for w in range(ways)]
+
+
+def first(k):
+    return sum(WIDTH[:k])
+
+
+def ways(sls):
+    return 1 << (len(sls) - 1).bit_length()
 
 
 def layout(core, T, topo):
     cores = T.cores
     N = len(cores)
 
-    def near(c):
-        return range(max(0, c - 2 * topo.CORES_PER_CHIP), c + 2 * topo.CORES_PER_CHIP + 1)
-
     def chip(c):
         return (topo.host(c), topo.chip(c))
 
-    relays, workers = [], []
+    helpers, workers = [], []
     for c in cores:
-        far = [d for d in near(c) if chip(d) == chip(c) or topo.mates(c, d)]
-        able = [d for d in far if d != c and all(topo.may_write(d, e) for e in cores if e != d)]
-        able.sort(key=lambda d: (chip(d) != chip(c), topo.die(d) == topo.die(c), d))
-        here, mate = [d for d in able if chip(d) == chip(c)], [d for d in able if chip(d) != chip(c)]
-        relays.append(here)
-        workers.append([here[0], here[2], mate[0], mate[2]])
-    mine = [r for r in range(N) if core == cores[r] or core in relays[r] or core in workers[r]]
+        near = range(max(0, c - 2 * topo.CORES_PER_CHIP), c + 2 * topo.CORES_PER_CHIP + 1)
+        here = [d for d in near if chip(d) == chip(c) and d != c]
+        mate = [d for d in near if topo.mates(c, d)]
+        for cs in (here, mate):
+            cs.sort(key=lambda d: (topo.die(d) == topo.die(c), d))
+
+        def able(d):
+            return all(topo.may_write(d, e) for e in cores if e != d)
+        here_p, mate_p = [d for d in here if able(d)], [d for d in mate if able(d)]
+        helpers.append(here_p + [d for d in here if not able(d)])
+        workers.append([here_p[0], mate_p[2], here_p[2], mate_p[0]])
+    mine = [r for r in range(N) if core == cores[r] or core in helpers[r] or core in workers[r]]
     if not mine:
         return None
     r = mine[0]
 
-    def host(q):
-        return [p for p in range(N) if topo.host(cores[p]) == topo.host(cores[q])]
-
     def kin(q):
-        own = host(q)
+        own = [p for p in range(N) if topo.host(cores[p]) == topo.host(cores[q])]
         oth = [p for p in range(N) if p not in own]
 
         def same(p):
             return topo.may_write(cores[q], cores[p])
-        return ([p for p in own if not same(p)], [p for p in own if p != q and same(p)],
+        return ([p for p in own if not same(p)], [p for p in own if p != q and same(p)][0],
                 [p for p in oth if not same(p)], [p for p in oth if same(p)])
 
-    def relay_jobs(q):
-        o, s, p, f = kin(q)
-        s = s[0]
-        return [[(0, FIRST, [(o[0], 0), (o[0], 1), (o[0], 2), (o[0], 3)]), (1, SECOND, [(s, 0), (s, 1)])],
-                [(0, FIRST, [(o[1], 0), (o[1], 1), (o[1], 2), (o[1], 3)]), (1, SECOND, [(s, 2), (s, 3)])],
-                [(0, FIRST, [(p[0], 0), (p[0], 1), (f[0], 2), (f[0], 3)]), (0, FIRST + 512, [(q, 2)])],
-                [(0, FIRST, [(p[1], 0), (p[1], 1), (f[1], 2), (f[1], 3)]), (0, FIRST + 512, [(q, 3)])]]
+    on = topo.mask(cores[r], helpers[r][0])
+    off = topo.mask(cores[r], cores[kin(r)[3][0]])
+    X, Y = sum(bits(on)[0::2]), sum(bits(on)[1::2])
+    M = {"on": on, "off": off, "rest": on & ~off, "X": X, "Y": Y, "X1": X & off, "X2": X & ~off, "Y1": Y & off, "Y2": Y & ~off}
 
-    def own_jobs(q):
+    def calls(q, h):
         o, s, p, f = kin(q)
-        return [[(f[0], 0), (f[0], 1), (p[0], 2), (p[0], 3)], [(f[1], 0), (f[1], 1), (p[1], 2), (p[1], 3)], [(q, 0), (q, 1)]]
+        e = 2 * h
+        V = [[(o[0], e), (o[1], e)], [(o[0], e + 1), (o[1], e + 1)], [(s, e + 1), (q, e + 1)], [(s, e), (q, e)]]
+        C = [[(d, e), (d, e + 1)] for d in (f[0], p[0], f[1], p[1])]
+        r0, c0, r1 = (0, V[0], "X"), (4, V[1], "X"), (1, V[2], "X")
+        r2, r3 = (2, [(f[0], e + 1), (p[0], e)], "Y"), (3, [(f[1], e + 1), (p[1], e)], "Y")
+        last = [(None, [(f[0], e)], "X1"), (None, [(p[1], e + 1)], "Y1"), (5, [(s, e)], "X2"), (None, [(q, e)], "Y2")]
+        if h == 0:
+            K = [(1, 0, [r0]), (2, 2, [c0, r2]), (3, 3, [(6, [(p[0], e + 1), (f[1], e)], "Y"), r1]), (4, 4, [r3])]
+        else:
+            K = [(2, 2, [c0, r2]), (3, 3, [(6, [(p[0], e + 1), (f[1], e)], "Y2"), r1]), (4, 4, [r3, r0])]
+        return V, C, K + [(4, 4, last)]
 
-    c = cores[r]
-    on = topo.mask(c, relays[r][0])
-    off = topo.mask(c, cores[kin(r)[3][0]])
-    own = host(r)
-    return {"r": r, "own": own, "oth": [p for p in range(N) if p not in own], "R": relays, "W": workers, "kin": kin,
-            "relay_jobs": relay_jobs, "own_jobs": own_jobs, "on": on, "off": off, "rest": on & ~off,
-            "hand": [[on, on] + split(on, 2), split(on & ~off, 2) + [0, 0]]}
+    def shares(q):
+        o, s, p, f = kin(q)
+        n, m = WIDTH[0] // 8, WIDTH[2] // 8
+        return {("H", 2): (0, p[0], 0, n), ("H", 3): (0, p[1], 0, n), ("H", 4): (0, f[0], 0, n), ("H", 5): (0, f[1], 0, n),
+                ("H", 0): (1, p[0], 0, m), ("H", 1): (1, p[1], 0, m), ("H", 6): (1, f[0], 0, m),
+                ("W", 1): (1, f[1], 0, m // 2), ("W", 3): (1, f[1], m // 2, m // 2)}
+
+    def passed(q, h):
+        out = [([], []) for x in helpers[q]]
+        for nv, ns, ts in calls(q, h)[2]:
+            for x, sls, m in ts:
+                if x is not None:
+                    out[x][0].extend(sls)
+                    out[x][1].append(count(M[m]))
+        return out
+
+    def reach(q, sl):
+        for h in range(2):
+            for sls, n in passed(q, h):
+                if sl in sls:
+                    return count(off) // ways(sls)
+            for nv, ns, ts in calls(q, h)[2]:
+                for x, sls, m in ts:
+                    if x is None and sl in sls:
+                        return count(M[m])
+
+    own = [p for p in range(N) if topo.host(cores[p]) == topo.host(cores[r])]
+    return {"r": r, "own": own, "oth": [p for p in range(N) if p not in own], "H": helpers[r], "W": workers, "kin": kin,
+            "calls": calls, "shares": shares, "passed": passed, "reach": reach, "M": M}
 
 
 def rank_program(g, core, T, topo):
@@ -93,168 +131,165 @@ def rank_program(g, core, T, topo):
         helper(g, core, T, topo, L)
 
 
-def copy(core, topo, dst, mask, sem, src_ap, dst_ap):
-    rid, pid = topo.addr(dst, core)
-    return count(mask), RemoteDMATransfer(dst_ids=[DstId(rid=rid, pnc=pid)], dma_engine_mask=mask, remote_sem=sem, src=src_ap, dst=dst_ap)
+def send(core, topo, dsts, mask, sem, src, landing):
+    ids = [topo.addr(d, core) for d in dsts]
+    return RemoteDMATransfer(dst_ids=[DstId(rid=rid, pnc=pid) for rid, pid in ids], dma_engine_mask=mask, remote_sem=sem,
+                             srcs=[src], dsts=[landing for d in dsts])
+
+
+def caller(g, S):
+    sent = [0]
+
+    def call(transfers, masks):
+        g.remote_dma_fused(transfers, local_sem=S.sent)
+        sent[0] += sum(count(m) for m in masks)
+    return sent, call
 
 
 def owner(g, core, T, topo, L):
-    S, cores, r, own, oth, R, W = T.sem, T.cores, L["r"], L["own"], L["oth"], L["R"], L["W"]
+    S, cores, r, own, oth, H, W, M = T.sem, T.cores, L["r"], L["own"], L["oth"], L["H"], L["W"], L["M"]
     i = own.index(r)
-    o, s, p, f = L["kin"](r)
-    s = s[0]
-    relay_jobs, own_jobs = L["relay_jobs"](r), L["own_jobs"](r)
+    plan = [L["calls"](r, h) for h in range(2)]
 
     for k in range(4):
         g.sync.dma_start(T.list[16 * k:16 * k + 16, :], T.idx[:]).then_inc(S.ix, 16)
         g.scalar.dma_start(T.list[16 * k + 64:16 * k + 80, :], T.idx[:]).then_inc(S.ix, 16)
     a = 0
     for k, n in enumerate(LOADS):
-        if k >= 2:
-            g.sync.wait_ge(S["t%d" % (k - 2)], 16)
+        if k == 1:
+            g.sync.wait_ge(S.go, 1)
         g.sync.dma_start(T.win[:, a:a + n], T.tab[:, a:a + n]).then_inc(S["t%d" % k], 16)
         a += n
 
-    seq = []
-    for job in relay_jobs[:2]:
-        seq += job[0][2]
-    for job in relay_jobs[2:]:
-        seq += job[0][2] + job[1][2]
-    for job in relay_jobs[:2]:
-        seq += job[1][2]
-    for job in own_jobs:
-        seq += job
-    pos = {sl: 128 * n for n, sl in enumerate(seq)}
+    seq = [sl for V, C, K in plan for pair in V + C for sl in pair]
+    pos = {sl: sum(WIDTH[k] for d, k in seq[:n]) for n, sl in enumerate(seq)}
 
     v, sc = g.vector, g.scalar
+    mine = [sl for sl in seq if sl[0] in own]
+    at = {(d, k): 128 + 32 * oth.index(d) + first(k) // 16 for d in oth for k in range(4)}
+    at.update({sl: sum(WIDTH[k] for d, k in mine[:n]) // 16 for n, sl in enumerate(mine)})
     v.wait_ge(S.ix, 128)
     v.tensor_scalar(out=T.tmp[:], in0=T.list[:], scalar1=8191, scalar2=None, op0=AluOpType.bitwise_and).then_inc(S.pre, 1)
     v.wait_ge(S.pre, 1)
-    v.tensor_copy(out=T.offs[:, 0:128], in_=T.tmp[:]).then_inc(S.pre, 1)
+    for d, k in mine:
+        b, n = 32 * own.index(d) + first(k) // 16, WIDTH[k] // 16
+        v.tensor_copy(out=T.offs[:, at[(d, k)]:at[(d, k)] + n], in_=T.tmp[:, b:b + n]).then_inc(S.pre, 1)
+    v.wait_ge(S.pre, 1 + len(mine))
     for q in (v, sc):
-        q.wait_ge(S.pre, 2)
         for k in range(len(LOADS)):
             q.wait_ge(S["t%d" % k], 16)
-    steps = [([(o[0], 0, 2)], [(o[0], 2, 2)]),
-             ([(o[1], 0, 2)], [(o[1], 2, 2)]),
-             ([(r, 2, 1), (p[0], 0, 2), (f[0], 2, 2)], [(r, 3, 1), (p[1], 0, 2), (f[1], 2, 2)]),
-             ([(s, 0, 2)], [(s, 2, 2)]),
-             ([(f[0], 0, 2)], [(p[0], 2, 2)]),
-             ([(f[1], 0, 2)], [(p[1], 2, 2)]),
-             ([(r, 0, 1)], [(r, 1, 1)])]
-    for q, side in ((v, 0), (sc, 1)):
-        waited = False
-        for n, step in enumerate(steps):
-            for d, k, many in step[side]:
-                if d in oth and not waited:
-                    q.wait_ge(S.oth, 32 if i < 2 else 64)
-                    waited = True
-                b = (32 * own.index(d) if d in own else 128 + 32 * oth.index(d)) + 8 * k
-                a = pos[(d, k)]
-                out, src = T.part[:, a:a + 128 * many], T.win[:, 0:8192].indirect(T.offs[:, b:b + 8 * many])
-                if side == 0:
-                    v.tensor_copy(out=out, in_=src).then_inc(S["st%d" % n], 1)
-                else:
-                    sc.activation(out=out, in_=src, func=ActivationFunctionType.Copy, bias=-0.0, scale=1.0).then_inc(S["st%d" % n], 1)
+    for h, (V, C, K) in enumerate(plan):
+        n = WIDTH[2 * h]
+        for pair in V:
+            a, b = pos[pair[0]], at[pair[0]]
+            v.tensor_copy(out=T.part[:, a:a + 2 * n], in_=T.win[:, 0:8192].indirect(T.offs[:, b:b + n // 8])).then_inc(S.vs, 1)
+        lists = [(x, d) for q in oth for x, d, c, m in L["shares"](q).values()]
+        sc.wait_ge((S.oe, S.ol)[h], count(M["off"]) * lists.count((h, r)))
+        for pair in C:
+            a, b = pos[pair[0]], at[pair[0]]
+            sc.activation(out=T.part[:, a:a + 2 * n], in_=T.win[:, 0:8192].indirect(T.offs[:, b:b + n // 8]),
+                          func=ActivationFunctionType.Copy, bias=-0.0, scale=1.0).then_inc(S.ss, 1)
 
-    sent = [0]
-
-    def call(pairs):
-        g.remote_dma_fused([t for n, t in pairs], local_sem=S.sent)
-        sent[0] += sum(n for n, t in pairs)
-
-    def quarter(q, to, mask):
-        b = 32 * own.index(q)
-        ids = [topo.addr(w, core) for w in to]
-        call([(count(mask), RemoteDMATransfer(
-            dst_ids=[DstId(rid=rid, pnc=pid) for rid, pid in ids], dma_engine_mask=mask, remote_sem=S.lst,
-            srcs=[T.list[:, b:b + 32]], dsts=[T.list[:, 0:32] for w in to]))])
-
-    partner = o[sorted([r, s]).index(r)]
+    sent, call = caller(g, S)
     g.wait_ge(S.ix, 128)
-    quarter(r, R[r], L["on"])
-    quarter(partner, W[partner][2:], L["off"])
-
-    def hand(k, n):
-        sls = [sl for which, base, job in relay_jobs[k] if which == n for sl in job]
-        a, to, cols = pos[sls[0]], (FIRST, SECOND)[n], 128 * len(sls)
-        return copy(core, topo, R[r][k], L["hand"][n][k], (S.ra, S.rb)[n], T.part[:, a:a + cols], T.part[:, to:to + cols])
-
-    def deliver(job, mask):
-        return [copy(core, topo, W[d][k], m, S.arr, T.part[:, pos[(d, k)]:pos[(d, k)] + 128], T.part[:, SLOT + 128 * r:SLOT + 128 * r + 128])
-                for (d, k), m in zip(job, split(mask, len(job)))]
-
-    calls = [[hand(0, 0)], [hand(1, 0)], [hand(2, 0), hand(3, 0)], [hand(0, 1), hand(1, 1)],
-             deliver(own_jobs[0], L["off"]), deliver(own_jobs[1], L["off"]), deliver(own_jobs[2], L["rest"])]
-    for n, pairs in enumerate(calls):
-        g.wait_ge(S["st%d" % n], sum(len(x) for x in steps[n]))
-        call(pairs)
+    b = 32 * i
+    call([send(core, topo, H[2:6], M["on"], S.lst, T.list[:, b:b + 32], T.list[:, 0:32])], [M["on"]])
+    g.sem_inc(S.go, 1)
+    for h, (V, C, K) in enumerate(plan):
+        w = WIDTH[2 * h]
+        filled = [PASS + 4 * WIDTH[0] * h for x in H]
+        for nv, ns, ts in K:
+            g.wait_ge(S.vs, len(V) * h + nv)
+            if len(C) * h + ns:
+                g.wait_ge(S.ss, len(C) * h + ns)
+            out = []
+            for x, sls, m in ts:
+                a, cols = pos[sls[0]], w * len(sls)
+                if x is None:
+                    d, k = sls[0]
+                    out.append(send(core, topo, [W[d][k]], M[m], S.arr, T.part[:, a:a + cols], T.part[:, SLOT + w * r:SLOT + w * r + w]))
+                else:
+                    out.append(send(core, topo, [H[x]], M[m], S["h%d" % h], T.part[:, a:a + cols], T.part[:, filled[x]:filled[x] + cols]))
+                    filled[x] += cols
+            call(out, [M[m] for x, sls, m in ts])
 
     for q, ks in ((g.sync, [i, i ^ 2]), (g.scalar, [i ^ 1, i ^ 3])):
-        for k in ks:
-            q.wait_ge(S["yq%d" % k], 16)
-            q.dma_start(T.y[:, 512 * k:512 * k + 512], T.yb[:, 512 * k:512 * k + 512]).then_inc(S.yd, 16)
+        for h in range(2):
+            for k in ks:
+                q.wait_ge(S["y%d" % (4 * h + k)], count(M["rest"] if k == i else M["off"]) + count(M["off"]))
+                a, w = 512 * k + first(2 * h), 2 * WIDTH[2 * h]
+                q.dma_start(T.y[:, a:a + w], T.yb[:, a:a + w]).then_inc(S.yd, 16)
     g.wait_ge(S.sent, sent[0])
-    g.wait_ge(S.yd, 64)
+    g.wait_ge(S.yd, 128)
 
 
 def helper(g, core, T, topo, L):
-    S, cores, r, own, oth, R, W = T.sem, T.cores, L["r"], L["own"], L["oth"], L["R"], L["W"]
+    S, cores, r, own, oth, H, W, M = T.sem, T.cores, L["r"], L["own"], L["oth"], L["H"], L["W"], L["M"]
+    on, off, rest = M["on"], M["off"], M["rest"]
     i = own.index(r)
     k = W[r].index(core) if core in W[r] else None
-    j = R[r].index(core) if core in R[r] else None
+    j = H.index(core) if core in H else None
     v = g.vector
-    sent = [0]
-
-    def call(pairs):
-        g.remote_dma_fused([t for n, t in pairs], local_sem=S.sent)
-        sent[0] += sum(n for n, t in pairs)
+    sent, call = caller(g, S)
 
     if k is not None:
-        g.iota(T.tmp[:, 32:40], [[0, 8]], 0, 1).then_inc(S.nums, 1)
-        g.iota(T.tmp[:, 40:48], [[16, 8]], 0, 0).then_inc(S.nums, 1)
-    v.wait_ge(S.lst, count(L["on"]) if j is not None else count(L["off"]))
-    v.tensor_scalar(out=T.tmp[:, 0:32], in0=T.list[:, 0:32], scalar1=8191, scalar2=None, op0=AluOpType.bitwise_and).then_inc(S.pre, 1)
+        w = WIDTH[k]
+        n = w // 16
+        g.iota(T.tmp[:, 32:32 + n], [[0, n]], 0, 1).then_inc(S.nums, 1)
+        g.iota(T.tmp[:, 48:48 + n], [[16, n]], 0, 0).then_inc(S.nums, 1)
+
+    onward = {2: [W[r][1], H[0]], 3: [W[r][3], H[1]], 4: [H[6]]}.get(j)
+    lst = count(on if j is not None and 2 <= j < 6 else off)
+    if onward:
+        g.wait_ge(S.lst, lst)
+        call([send(core, topo, onward, off, S.lst, T.list[:, 0:32], T.list[:, 0:32])], [off])
+    h, d, a, m = L["shares"](r)[("H", j) if j is not None else ("W", k)]
+    a += first(2 * h) // 16
+    v.wait_ge(S.lst, lst)
+    v.tensor_scalar(out=T.tmp[:, 0:m], in0=T.list[:, a:a + m], scalar1=8191, scalar2=None, op0=AluOpType.bitwise_and).then_inc(S.pre, 1)
     v.wait_ge(S.pre, 1)
-    v.tensor_copy(out=T.offs[:, 0:32], in_=T.tmp[:, 0:32]).then_inc(S.pre, 1)
-    d, a, n = {(0, 0): (0, 0, 32), (2, 1): (1, 0, 32), (1, None): (2, 0, 16), (3, None): (2, 16, 16),
-               (None, 2): (3, 0, 16), (None, 3): (3, 16, 16)}[(j, k)]
+    v.tensor_copy(out=T.offs[:, 0:m], in_=T.tmp[:, 0:m]).then_inc(S.pre, 1)
     g.wait_ge(S.pre, 2)
-    to = 128 + 32 * i + a
-    call([copy(core, topo, cores[oth[d]], L["off"], S.oth, T.offs[:, a:a + n], T.offs[:, to:to + n])])
+    a += 128 + 32 * i
+    call([send(core, topo, [cores[d]], off, (S.oe, S.ol)[h], T.offs[:, 0:m], T.offs[:, a:a + m])], [off])
 
     if k is not None:
-        v.wait_ge(S.nums, 2)
+        a = first(k) // 16
+
+        def t(x):
+            return T.tmp[:, 32 + 16 * x:32 + 16 * x + n]
         ops = [
-            lambda: v.tensor_scalar(out=T.tmp[:, 48:56], in0=T.tmp[:, 32:40], scalar1=15, scalar2=None, op0=AluOpType.bitwise_and),
-            lambda: v.tensor_tensor(out=T.tmp[:, 56:64], in0=T.tmp[:, 48:56], in1=T.tmp[:, 40:48], op=AluOpType.add),
-            lambda: v.tensor_scalar(out=T.tmp[:, 64:72], in0=T.list[:, 8 * k:8 * k + 8], scalar1=13, scalar2=None, op0=AluOpType.logical_shift_right),
-            lambda: v.tensor_scalar(out=T.tmp[:, 72:80], in0=T.tmp[:, 64:72], scalar1=128, scalar2=None, op0=AluOpType.mult),
-            lambda: v.tensor_tensor(out=T.tmp[:, 80:88], in0=T.tmp[:, 72:80], in1=T.tmp[:, 56:64], op=AluOpType.add),
-            lambda: v.tensor_copy(out=T.offs[:, 32:40], in_=T.tmp[:, 80:88]),
+            lambda: v.tensor_scalar(out=t(2), in0=t(0), scalar1=15, scalar2=None, op0=AluOpType.bitwise_and),
+            lambda: v.tensor_tensor(out=t(3), in0=t(2), in1=t(1), op=AluOpType.add),
+            lambda: v.tensor_scalar(out=t(0), in0=T.list[:, a:a + n], scalar1=13, scalar2=None, op0=AluOpType.logical_shift_right),
+            lambda: v.tensor_scalar(out=t(4), in0=t(0), scalar1=w, scalar2=None, op0=AluOpType.mult),
+            lambda: v.tensor_tensor(out=t(5), in0=t(4), in1=t(3), op=AluOpType.add),
+            lambda: v.tensor_copy(out=T.offs[:, 32:32 + n], in_=t(5)),
         ]
-        for n, op in enumerate(ops):
+        v.wait_ge(S.nums, 2)
+        for x, op in enumerate(ops):
             op().then_inc(S.sof, 1)
-            v.wait_ge(S.sof, n + 1)
-        total = 0
-        for q in own + oth:
-            for job in L["relay_jobs"](q):
-                total += sum(count(L["off"]) // len(sls) for which, base, sls in job if (r, k) in sls)
-            total += sum(count(L["off"]) // len(sls) for sls in L["own_jobs"](q)[:2] if (r, k) in sls)
-            total += sum(count(L["rest"]) // len(sls) for sls in L["own_jobs"](q)[2:] if (r, k) in sls)
-        v.wait_ge(S.arr, total)
-        v.tensor_copy(out=T.part[:, PICK:PICK + 128], in_=T.part[:, SLOT:SLOT + 1024].indirect(T.offs[:, 32:40])).then_inc(S.pick, 1)
+            v.wait_ge(S.sof, x + 1)
+        v.wait_ge(S.arr, sum(L["reach"](q, (r, k)) for q in own + oth))
+        v.tensor_copy(out=T.part[:, PICK:PICK + w], in_=T.part[:, SLOT:SLOT + 8 * w].indirect(T.offs[:, 32:32 + n])).then_inc(S.pick, 1)
 
     if j is not None:
-        for which, base, sls in L["relay_jobs"](r)[j]:
-            g.wait_ge((S.ra, S.rb)[which], count(L["hand"][which][j]))
-            call([copy(core, topo, W[d][e], m, S.arr, T.part[:, base + 128 * x:base + 128 * x + 128], T.part[:, SLOT + 128 * r:SLOT + 128 * r + 128])
-                  for x, ((d, e), m) in enumerate(zip(sls, split(L["off"], len(sls))))])
+        for h in range(2):
+            sls, ns = L["passed"](r, h)[j]
+            g.wait_ge(S["h%d" % h], sum(ns))
+            base, c, ms = PASS + 4 * WIDTH[0] * h, WIDTH[2 * h], split(off, ways(sls))[:len(sls)]
+            call([send(core, topo, [W[d][e]], m, S.arr, T.part[:, base + c * x:base + c * x + c], T.part[:, SLOT + c * r:SLOT + c * r + c])
+                  for x, ((d, e), m) in enumerate(zip(sls, ms))], ms)
 
     if k is not None:
-        a = 512 * i + 128 * k
+        a = 512 * i + first(k)
         g.wait_ge(S.pick, 1)
-        for pair in ((i, i ^ 1), (i ^ 2, i ^ 3)):
-            call([copy(core, topo, cores[own[q]], m, S["yq%d" % i], T.part[:, PICK:PICK + 128], T.yb[:, a:a + 128])
-                  for q, m in zip(pair, split(L["off"], 2))])
+
+        def give(xs, mask):
+            return send(core, topo, [cores[own[i ^ x]] for x in xs], mask, S["y%d" % (4 * (k // 2) + i)],
+                        T.part[:, PICK:PICK + w], T.yb[:, a:a + w])
+        if j is not None:
+            call([give((2, 1, 3), off), give((0,), rest)], [off, rest])
+        else:
+            call([give((0, 1, 2, 3), off)], [off])
     g.wait_ge(S.sent, sent[0])

from concourse.bass import DstId, RemoteDMATransfer
from concourse.mybir import AluOpType, ActivationFunctionType

WIDTH = [160, 160, 96, 96]
LOADS = [3840, 4352]
SLOT, PASS, PICK = 0, 1280, 2560
SCRATCH = {
    "win": ("sbuf", [128, 8192], "float32"),
    "part": ("sbuf", [128, 4096], "float32"),
    "yb": ("sbuf", [128, 2048], "float32"),
    "list": ("sbuf", [128, 128], "int32"),
    "tmp": ("sbuf", [128, 128], "int32"),
    "offs": ("sbuf", [128, 256], "uint16"),
}
SEMAPHORES = (["ix", "go", "pre", "oe", "ol", "sent", "yd", "lst", "nums", "sof", "arr", "pick", "h0", "h1", "vs", "ss"]
              + ["t%d" % k for k in range(len(LOADS))] + ["y%d" % k for k in range(8)])


def count(mask):
    return bin(mask).count("1")


def bits(mask):
    return [1 << b for b in range(32) if mask >> b & 1]


def split(mask, ways):
    n = count(mask) // ways
    return [sum(bits(mask)[n * w:n * w + n]) for w in range(ways)]


def first(k):
    return sum(WIDTH[:k])


def ways(sls):
    return 1 << (len(sls) - 1).bit_length()


def layout(core, T, topo):
    cores = T.cores
    N = len(cores)

    def chip(c):
        return (topo.host(c), topo.chip(c))

    helpers, workers = [], []
    for c in cores:
        near = range(max(0, c - 2 * topo.CORES_PER_CHIP), c + 2 * topo.CORES_PER_CHIP + 1)
        here = [d for d in near if chip(d) == chip(c) and d != c]
        mate = [d for d in near if topo.mates(c, d)]
        for cs in (here, mate):
            cs.sort(key=lambda d: (topo.die(d) == topo.die(c), d))

        def able(d):
            return all(topo.may_write(d, e) for e in cores if e != d)
        here_p, mate_p = [d for d in here if able(d)], [d for d in mate if able(d)]
        helpers.append(here_p + [d for d in here if not able(d)])
        workers.append([here_p[0], mate_p[2], here_p[2], mate_p[0]])
    mine = [r for r in range(N) if core == cores[r] or core in helpers[r] or core in workers[r]]
    if not mine:
        return None
    r = mine[0]

    def kin(q):
        own = [p for p in range(N) if topo.host(cores[p]) == topo.host(cores[q])]
        oth = [p for p in range(N) if p not in own]

        def same(p):
            return topo.may_write(cores[q], cores[p])
        return ([p for p in own if not same(p)], [p for p in own if p != q and same(p)][0],
                [p for p in oth if not same(p)], [p for p in oth if same(p)])

    on = topo.mask(cores[r], helpers[r][0])
    off = topo.mask(cores[r], cores[kin(r)[3][0]])
    X, Y = sum(bits(on)[0::2]), sum(bits(on)[1::2])
    M = {"on": on, "off": off, "rest": on & ~off, "X": X, "Y": Y, "X1": X & off, "X2": X & ~off, "Y1": Y & off, "Y2": Y & ~off}

    def calls(q, h):
        o, s, p, f = kin(q)
        e = 2 * h
        V = [[(o[0], e), (o[1], e)], [(o[0], e + 1), (o[1], e + 1)], [(s, e + 1), (q, e + 1)], [(s, e), (q, e)]]
        C = [[(d, e), (d, e + 1)] for d in (f[0], p[0], f[1], p[1])]
        r0, c0, r1 = (0, V[0], "X"), (4, V[1], "X"), (1, V[2], "X")
        r2, r3 = (2, [(f[0], e + 1), (p[0], e)], "Y"), (3, [(f[1], e + 1), (p[1], e)], "Y")
        last = [(None, [(f[0], e)], "X1"), (None, [(p[1], e + 1)], "Y1"), (5, [(s, e)], "X2"), (None, [(q, e)], "Y2")]
        if h == 0:
            K = [(1, 0, [r0]), (2, 2, [c0, r2]), (3, 3, [(6, [(p[0], e + 1), (f[1], e)], "Y"), r1]), (4, 4, [r3])]
        else:
            K = [(2, 2, [c0, r2]), (3, 3, [(6, [(p[0], e + 1), (f[1], e)], "Y2"), r1]), (4, 4, [r3, r0])]
        return V, C, K + [(4, 4, last)]

    def shares(q):
        o, s, p, f = kin(q)
        n, m = WIDTH[0] // 8, WIDTH[2] // 8
        return {("H", 2): (0, p[0], 0, n), ("H", 3): (0, p[1], 0, n), ("H", 4): (0, f[0], 0, n), ("H", 5): (0, f[1], 0, n),
                ("H", 0): (1, p[0], 0, m), ("H", 1): (1, p[1], 0, m), ("H", 6): (1, f[0], 0, m),
                ("W", 1): (1, f[1], 0, m // 2), ("W", 3): (1, f[1], m // 2, m // 2)}

    def passed(q, h):
        out = [([], []) for x in helpers[q]]
        for nv, ns, ts in calls(q, h)[2]:
            for x, sls, m in ts:
                if x is not None:
                    out[x][0].extend(sls)
                    out[x][1].append(count(M[m]))
        return out

    def reach(q, sl):
        for h in range(2):
            for sls, n in passed(q, h):
                if sl in sls:
                    return count(off) // ways(sls)
            for nv, ns, ts in calls(q, h)[2]:
                for x, sls, m in ts:
                    if x is None and sl in sls:
                        return count(M[m])

    own = [p for p in range(N) if topo.host(cores[p]) == topo.host(cores[r])]
    return {"r": r, "own": own, "oth": [p for p in range(N) if p not in own], "H": helpers[r], "W": workers, "kin": kin,
            "calls": calls, "shares": shares, "passed": passed, "reach": reach, "M": M}


def rank_program(g, core, T, topo):
    L = layout(core, T, topo)
    if L is None:
        return
    if core == T.cores[L["r"]]:
        owner(g, core, T, topo, L)
    else:
        helper(g, core, T, topo, L)


def send(core, topo, dsts, mask, sem, src, landing):
    ids = [topo.addr(d, core) for d in dsts]
    return RemoteDMATransfer(dst_ids=[DstId(rid=rid, pnc=pid) for rid, pid in ids], dma_engine_mask=mask, remote_sem=sem,
                             srcs=[src], dsts=[landing for d in dsts])


def caller(g, S):
    sent = [0]

    def call(transfers, masks):
        g.remote_dma_fused(transfers, local_sem=S.sent)
        sent[0] += sum(count(m) for m in masks)
    return sent, call


def owner(g, core, T, topo, L):
    S, cores, r, own, oth, H, W, M = T.sem, T.cores, L["r"], L["own"], L["oth"], L["H"], L["W"], L["M"]
    i = own.index(r)
    plan = [L["calls"](r, h) for h in range(2)]

    for k in range(4):
        g.sync.dma_start(T.list[16 * k:16 * k + 16, :], T.idx[:]).then_inc(S.ix, 16)
        g.scalar.dma_start(T.list[16 * k + 64:16 * k + 80, :], T.idx[:]).then_inc(S.ix, 16)
    a = 0
    for k, n in enumerate(LOADS):
        if k == 1:
            g.sync.wait_ge(S.go, 1)
        g.sync.dma_start(T.win[:, a:a + n], T.tab[:, a:a + n]).then_inc(S["t%d" % k], 16)
        a += n

    seq = [sl for V, C, K in plan for pair in V + C for sl in pair]
    pos = {sl: sum(WIDTH[k] for d, k in seq[:n]) for n, sl in enumerate(seq)}

    v, sc = g.vector, g.scalar
    mine = [sl for sl in seq if sl[0] in own]
    at = {(d, k): 128 + 32 * oth.index(d) + first(k) // 16 for d in oth for k in range(4)}
    at.update({sl: sum(WIDTH[k] for d, k in mine[:n]) // 16 for n, sl in enumerate(mine)})
    v.wait_ge(S.ix, 128)
    v.tensor_scalar(out=T.tmp[:], in0=T.list[:], scalar1=8191, scalar2=None, op0=AluOpType.bitwise_and).then_inc(S.pre, 1)
    v.wait_ge(S.pre, 1)
    for d, k in mine:
        b, n = 32 * own.index(d) + first(k) // 16, WIDTH[k] // 16
        v.tensor_copy(out=T.offs[:, at[(d, k)]:at[(d, k)] + n], in_=T.tmp[:, b:b + n]).then_inc(S.pre, 1)
    v.wait_ge(S.pre, 1 + len(mine))
    for q in (v, sc):
        for k in range(len(LOADS)):
            q.wait_ge(S["t%d" % k], 16)
    for h, (V, C, K) in enumerate(plan):
        n = WIDTH[2 * h]
        for pair in V:
            a, b = pos[pair[0]], at[pair[0]]
            v.tensor_copy(out=T.part[:, a:a + 2 * n], in_=T.win[:, 0:8192].indirect(T.offs[:, b:b + n // 8])).then_inc(S.vs, 1)
        lists = [(x, d) for q in oth for x, d, c, m in L["shares"](q).values()]
        sc.wait_ge((S.oe, S.ol)[h], count(M["off"]) * lists.count((h, r)))
        for pair in C:
            a, b = pos[pair[0]], at[pair[0]]
            sc.activation(out=T.part[:, a:a + 2 * n], in_=T.win[:, 0:8192].indirect(T.offs[:, b:b + n // 8]),
                          func=ActivationFunctionType.Copy, bias=-0.0, scale=1.0).then_inc(S.ss, 1)

    sent, call = caller(g, S)
    g.wait_ge(S.ix, 128)
    b = 32 * i
    call([send(core, topo, H[2:6], M["on"], S.lst, T.list[:, b:b + 32], T.list[:, 0:32])], [M["on"]])
    g.sem_inc(S.go, 1)
    for h, (V, C, K) in enumerate(plan):
        w = WIDTH[2 * h]
        filled = [PASS + 4 * WIDTH[0] * h for x in H]
        for nv, ns, ts in K:
            g.wait_ge(S.vs, len(V) * h + nv)
            if len(C) * h + ns:
                g.wait_ge(S.ss, len(C) * h + ns)
            out = []
            for x, sls, m in ts:
                a, cols = pos[sls[0]], w * len(sls)
                if x is None:
                    d, k = sls[0]
                    out.append(send(core, topo, [W[d][k]], M[m], S.arr, T.part[:, a:a + cols], T.part[:, SLOT + w * r:SLOT + w * r + w]))
                else:
                    out.append(send(core, topo, [H[x]], M[m], S["h%d" % h], T.part[:, a:a + cols], T.part[:, filled[x]:filled[x] + cols]))
                    filled[x] += cols
            call(out, [M[m] for x, sls, m in ts])

    for q, ks in ((g.sync, [i, i ^ 2]), (g.scalar, [i ^ 1, i ^ 3])):
        for h in range(2):
            for k in ks:
                q.wait_ge(S["y%d" % (4 * h + k)], count(M["rest"] if k == i else M["off"]) + count(M["off"]))
                a, w = 512 * k + first(2 * h), 2 * WIDTH[2 * h]
                q.dma_start(T.y[:, a:a + w], T.yb[:, a:a + w]).then_inc(S.yd, 16)
    g.wait_ge(S.sent, sent[0])
    g.wait_ge(S.yd, 128)


def helper(g, core, T, topo, L):
    S, cores, r, own, oth, H, W, M = T.sem, T.cores, L["r"], L["own"], L["oth"], L["H"], L["W"], L["M"]
    on, off, rest = M["on"], M["off"], M["rest"]
    i = own.index(r)
    k = W[r].index(core) if core in W[r] else None
    j = H.index(core) if core in H else None
    v = g.vector
    sent, call = caller(g, S)

    if k is not None:
        w = WIDTH[k]
        n = w // 16
        g.iota(T.tmp[:, 32:32 + n], [[0, n]], 0, 1).then_inc(S.nums, 1)
        g.iota(T.tmp[:, 48:48 + n], [[16, n]], 0, 0).then_inc(S.nums, 1)

    onward = {2: [W[r][1], H[0]], 3: [W[r][3], H[1]], 4: [H[6]]}.get(j)
    lst = count(on if j is not None and 2 <= j < 6 else off)
    if onward:
        g.wait_ge(S.lst, lst)
        call([send(core, topo, onward, off, S.lst, T.list[:, 0:32], T.list[:, 0:32])], [off])
    h, d, a, m = L["shares"](r)[("H", j) if j is not None else ("W", k)]
    a += first(2 * h) // 16
    v.wait_ge(S.lst, lst)
    v.tensor_scalar(out=T.tmp[:, 0:m], in0=T.list[:, a:a + m], scalar1=8191, scalar2=None, op0=AluOpType.bitwise_and).then_inc(S.pre, 1)
    v.wait_ge(S.pre, 1)
    v.tensor_copy(out=T.offs[:, 0:m], in_=T.tmp[:, 0:m]).then_inc(S.pre, 1)
    g.wait_ge(S.pre, 2)
    a += 128 + 32 * i
    call([send(core, topo, [cores[d]], off, (S.oe, S.ol)[h], T.offs[:, 0:m], T.offs[:, a:a + m])], [off])

    if k is not None:
        a = first(k) // 16

        def t(x):
            return T.tmp[:, 32 + 16 * x:32 + 16 * x + n]
        ops = [
            lambda: v.tensor_scalar(out=t(2), in0=t(0), scalar1=15, scalar2=None, op0=AluOpType.bitwise_and),
            lambda: v.tensor_tensor(out=t(3), in0=t(2), in1=t(1), op=AluOpType.add),
            lambda: v.tensor_scalar(out=t(0), in0=T.list[:, a:a + n], scalar1=13, scalar2=None, op0=AluOpType.logical_shift_right),
            lambda: v.tensor_scalar(out=t(4), in0=t(0), scalar1=w, scalar2=None, op0=AluOpType.mult),
            lambda: v.tensor_tensor(out=t(5), in0=t(4), in1=t(3), op=AluOpType.add),
            lambda: v.tensor_copy(out=T.offs[:, 32:32 + n], in_=t(5)),
        ]
        v.wait_ge(S.nums, 2)
        for x, op in enumerate(ops):
            op().then_inc(S.sof, 1)
            v.wait_ge(S.sof, x + 1)
        v.wait_ge(S.arr, sum(L["reach"](q, (r, k)) for q in own + oth))
        v.tensor_copy(out=T.part[:, PICK:PICK + w], in_=T.part[:, SLOT:SLOT + 8 * w].indirect(T.offs[:, 32:32 + n])).then_inc(S.pick, 1)

    if j is not None:
        for h in range(2):
            sls, ns = L["passed"](r, h)[j]
            g.wait_ge(S["h%d" % h], sum(ns))
            base, c, ms = PASS + 4 * WIDTH[0] * h, WIDTH[2 * h], split(off, ways(sls))[:len(sls)]
            call([send(core, topo, [W[d][e]], m, S.arr, T.part[:, base + c * x:base + c * x + c], T.part[:, SLOT + c * r:SLOT + c * r + c])
                  for x, ((d, e), m) in enumerate(zip(sls, ms))], ms)

    if k is not None:
        a = 512 * i + first(k)
        g.wait_ge(S.pick, 1)

        def give(xs, mask):
            return send(core, topo, [cores[own[i ^ x]] for x in xs], mask, S["y%d" % (4 * (k // 2) + i)],
                        T.part[:, PICK:PICK + w], T.yb[:, a:a + w])
        if j is not None:
            call([give((2, 1, 3), off), give((0,), rest)], [off, rest])
        else:
            call([give((0, 1, 2, 3), off)], [off])
    g.wait_ge(S.sent, sent[0])
